import numpy as np
import ml_dtypes


def mxq(x, axis, fmt="e4m3"):
    dtype, down = {"e4m3": (ml_dtypes.float8_e4m3fn, 7), "e5m2": (ml_dtypes.float8_e5m2, 14)}[fmt]
    v = np.moveaxis(np.asarray(x, np.float32).astype(ml_dtypes.bfloat16).astype(np.float64), axis, -1)
    blocks = v.reshape(v.shape[:-1] + (-1, 32))
    amax = np.abs(blocks).max(-1, keepdims=True)
    byte = np.maximum(np.where(amax > 0, np.frexp(amax)[1] - 1 + 127, 0) - down, 1)
    scale = np.exp2(byte - 127.0)
    codes = (blocks / scale).astype(np.float32).astype(dtype).astype(np.float64)
    return np.moveaxis((codes * scale).reshape(v.shape), -1, axis)


WIDE = False


def mx_kscale(k):
    if not WIDE:
        return np.ones(k)
    levels = np.array([10, -10, 5, -5, 0])
    if k % 512:
        return np.exp2(np.random.permutation(np.resize(levels, k // 32))).repeat(32)
    a = np.empty((k // 512, 16))
    for p in range(k // 512):
        a[p, :8] = np.random.permutation(np.resize(levels, 8))
        for g in range(8):
            far = levels[np.abs(levels - a[p, g]) >= 10]
            a[p, g + 8] = far[np.random.randint(len(far))]
    return np.exp2(a.ravel()).repeat(32)


def f64(x):
    return np.asarray(x).astype(np.float64)


def striped(idx):
    return np.tile(idx.reshape(-1, 16).T, (8, 1)).astype(np.uint16)


def unstriped(offs):
    return offs[:16].T.reshape(-1).astype(np.int64)


def pack_weight(w):
    k, n = w.shape
    w = f64(np.asarray(w, np.float32).astype(ml_dtypes.bfloat16)).reshape(k // 32, 32, n)
    amax = np.abs(w).max(1)
    byte = np.clip(np.where(amax > 0, np.frexp(amax)[1] - 1 + 127 - 7, 1), 1, 254)
    scaled = (w * np.exp2(127.0 - byte)[:, None, :]).reshape(k, n).astype(np.float32)
    words = np.ascontiguousarray(scaled.reshape(k // 512, 128, 4, n).transpose(0, 1, 3, 2)).astype(ml_dtypes.float8_e4m3fn).view(np.uint8)
    return words, np.ascontiguousarray(byte.astype(np.uint8).reshape(k // 512, 16, n))


def unpack_weight(words, scales):
    g, p, n, _ = words.shape
    vals = np.ascontiguousarray(words).view(ml_dtypes.float8_e4m3fn).astype(np.float64) * np.repeat(np.exp2(scales.astype(np.float64) - 127.0), 8, axis=1)[..., None]
    return vals.transpose(0, 1, 3, 2).reshape(g * 512, n)


K, T, S, N, U = 512, 1024, 512, 128, 512
P = 2 ** 7


def setup_inputs():
    n = np.random.standard_normal
    s = mx_kscale(K)[:, None]
    packed_xT = pack_weight(n((K, T)) * s)
    return {
        "x_words": packed_xT[0],
        "x_scales": packed_xT[1],
        "w1": (n((K, N)) / np.sqrt(K) / s).astype(np.float32),
        "w2": (n((K, N)) / np.sqrt(K) / s).astype(np.float32),
        "w3": (n((K, N)) / np.sqrt(K) / s).astype(np.float32),
        "chg": (np.tile(np.random.uniform(0.3, 1.0, S) * np.where(np.random.uniform(size=S) < 0.5, 1.0, -1.0), (P, 1))).astype(np.float32),
        "offs": striped(np.random.permutation(T)[:S]),
        "ia": striped(np.random.randint(0, S, U)),
        "ib": striped(np.random.randint(0, S, U)),
    }


def reference(x_words, x_scales, w1, w2, w3, chg, offs, ia, ib):
    xq = unpack_weight(x_words, x_scales)[:, unstriped(offs)]
    y = mxq(f64(w1), 0, "e4m3").T @ xq
    dx = y[:, unstriped(ia)] - y[:, unstriped(ib)]
    z = mxq(f64(w2), 0, "e4m3").T @ xq
    dy = z[:, unstriped(ia)] - z[:, unstriped(ib)]
    rsq = (dx) ** 2 + (dy) ** 2 + 0.1
    yr = mxq(f64(w3), 0, "e4m3").T @ xq
    born = np.log(np.exp(yr) + 1.0) + 0.4
    ab = born[:, unstriped(ia)] * born[:, unstriped(ib)]
    ex = np.exp(-0.25 * (rsq / ab))
    fsq = rsq + ab * ex
    en = ((f64(chg)[:1][:, unstriped(ia)]) * (f64(chg)[:1][:, unstriped(ib)])) / np.sqrt(fsq)
    return -1.0 * en

@@ -1,0 +1,115 @@
+from contextlib import ExitStack
+
+import concourse.mybir as mybir
+
+K, T, S, N, U = 512, 1024, 512, 128, 512
+FLOPS = 3 * 2 * K * N * S
+
+F32 = mybir.dt.float32
+BF16 = mybir.dt.bfloat16
+I32 = mybir.dt.int32
+U32 = mybir.dt.uint32
+U16 = mybir.dt.uint16
+U8 = mybir.dt.uint8
+FP8X4 = mybir.dt.float8_e4m3fn_x4
+ALU = mybir.AluOpType
+ACT = mybir.ActivationFunctionType
+
+P = 128
+PACK = 4
+HALF = U // 2
+EXP_CAP = 2.0 ** 60
+
+
+def tile_picked_ygborn_en_p_kernel(tc, x_words, x_scales, w1, w2, w3, chg, offs, ia, ib, out):
+    nc = tc.nc
+    with ExitStack() as ctx:
+        sb = ctx.enter_context(tc.tile_pool(name="sb", bufs=1))
+        ps = ctx.enter_context(tc.psum_pool(name="ps", bufs=1))
+
+        def f32(name, width=U):
+            return sb.tile([P, width], F32, name=name, align_bytes=64)
+
+        offs_t = sb.tile([P, S // 16], U16, name="offs_t")
+        ia_t = sb.tile([P, U // 16], U16, name="ia_t")
+        ib_t = sb.tile([P, U // 16], U16, name="ib_t")
+        words = sb.tile([P, T], U32, name="words", align_bytes=64)
+        scales = sb.tile([P, T], U8, name="scales", align_bytes=64)
+        raw = {n: sb.tile([P, PACK, N], F32, name="raw" + n, align_bytes=64) for n in "312"}
+        q = f32("q")
+
+        nc.gpsimd.memset(scales[:].bitcast(I32), 0)
+        nc.sync.dma_start(offs_t[:], offs)
+        nc.sync.dma_start(words[:].bitcast(I32), x_words[0].rearrange("p n t -> p (n t)").bitcast(I32))
+        for r in range(4):
+            nc.scalar.dma_start(scales[r:P:32, :].bitcast(I32), x_scales[0, r:16:4, :].bitcast(I32))
+        for n, w in (("3", w3), ("1", w1), ("2", w2)):
+            nc.sync.dma_start(raw[n][:], w.rearrange("(p j) c -> p j c", j=PACK))
+        nc.sync.dma_start(ia_t[:], ia)
+        nc.sync.dma_start(q[:], chg)
+        nc.sync.dma_start(ib_t[:], ib)
+
+        xs = sb.tile([P, S], U8, name="xs", align_bytes=64)
+        xw = sb.tile([P, S], U32, name="xw", align_bytes=64)
+        nc.vector.tensor_copy(xs[:], scales[:].indirect(offs_t[:]))
+        nc.vector.tensor_copy(xw[:], words[:].indirect(offs_t[:]))
+
+        acc = {}
+        for n in "312":
+            grouped = sb.tile([P, N, PACK], BF16, name="grouped" + n, align_bytes=64)
+            cast = nc.vector.tensor_copy if n == "2" else nc.scalar.copy
+            cast(grouped[:], raw[n][:].rearrange("p j c -> p c j"))
+            codes = sb.tile([P, N], U32, name="codes" + n, align_bytes=64)
+            plane = sb.tile([P, N], U8, name="plane" + n, align_bytes=64)
+            nc.vector.quantize_mx(out=codes[:].bitcast(FP8X4), scales=plane[:], in_=grouped[:].rearrange("p c j -> p (c j)"))
+            acc[n] = ps.tile([P, S], F32, name="acc" + n)
+            nc.tensor.matmul_mx(out=acc[n][:], lhsT=codes[:].bitcast(FP8X4), lhsT_scale=plane[:],
+                                rhs=xw[:].bitcast(FP8X4), rhs_scale=xs[:], start=True, stop=True)
+
+        halves = [slice(0, HALF), slice(HALF, U)]
+        lists = [slice(0, HALF // 16), slice(HALF // 16, U // 16)]
+
+        def pair(window, op, name):
+            first = f32(name + "_b")
+            both = f32(name)
+            for h in range(2):
+                nc.vector.tensor_copy(first[:, halves[h]], window[:].indirect(ib_t[:, lists[h]]))
+            for h in range(2):
+                nc.vector.tensor_tensor(both[:, halves[h]], window[:].indirect(ia_t[:, lists[h]]), first[:, halves[h]], op)
+            return both
+
+        y, z, e, ec, sp, top, lb = (f32(n) for n in ("y", "z", "e", "ec", "sp", "top", "lb"))
+        nc.scalar.activation(e[:], acc["3"][:], ACT.Exp)
+        nc.scalar.copy(y[:], acc["1"][:])
+        nc.scalar.copy(z[:], acc["2"][:])
+        nc.vector.tensor_scalar(ec[:], e[:], EXP_CAP, None, ALU.min)
+        dx = pair(y, ALU.subtract, "dx")
+        for h in halves:
+            nc.scalar.activation(sp[:, h], ec[:, h], ACT.Ln, bias=1.0)
+        for h in halves:
+            nc.vector.tensor_tensor(top[:, h], acc["3"][:, h], sp[:, h], ALU.max)
+        for h in halves:
+            nc.scalar.activation(lb[:, h], top[:, h], ACT.Ln, bias=0.4)
+        dy = pair(z, ALU.subtract, "dy")
+        s = pair(lb, ALU.add, "s")
+
+        dx2, dy2, rsq, inv, t, v, w, fsq, r, res = (
+            f32(n) for n in ("dx2", "dy2", "rsq", "inv", "t", "v", "w", "fsq", "r", "res"))
+        nc.scalar.activation(dx2[:], dx[:], ACT.Square)
+        nc.scalar.activation(dy2[:], dy[:], ACT.Square)
+        nc.vector.scalar_tensor_tensor(rsq[:], dx2[:], 0.1, dy2[:], ALU.add, ALU.add)
+        for h in halves:
+            nc.scalar.activation(inv[:, h], s[:, h], ACT.Exp, scale=-1.0)
+        for h in halves:
+            nc.vector.scalar_tensor_tensor(t[:, h], rsq[:, h], -0.25, inv[:, h], ALU.mult, ALU.mult)
+        for h in halves:
+            nc.vector.tensor_tensor(v[:, h], t[:, h], s[:, h], ALU.add)
+        for h in halves:
+            nc.scalar.activation(w[:, h], v[:, h], ACT.Exp)
+        for h in halves:
+            nc.vector.tensor_tensor(fsq[:, h], w[:, h], rsq[:, h], ALU.add)
+        qq = pair(q, ALU.mult, "qq")
+        for h in halves:
+            nc.scalar.activation(r[:, h], fsq[:, h], ACT.Abs_reciprocal_sqrt)
+            nc.vector.scalar_tensor_tensor(res[:, h], r[:, h], -1.0, qq[:, h], ALU.mult, ALU.mult)
+            nc.sync.dma_start(out[:, h], res[:, h])

@@ -35,81 +35,117 @@ def tile_picked_ygborn_en_p_kernel(tc, x_words, x_scales, w1, w2, w3, chg, offs,
         ib_t = sb.tile([P, U // 16], U16, name="ib_t")
         words = sb.tile([P, T], U32, name="words", align_bytes=64)
         scales = sb.tile([P, T], U8, name="scales", align_bytes=64)
-        raw = {n: sb.tile([P, PACK, N], F32, name="raw" + n, align_bytes=64) for n in "312"}
+        raw = {n: sb.tile([P, PACK, N], F32, name="raw" + n, tag="raw" + n, align_bytes=64) for n in "312"}
         q = f32("q")
 
-        nc.gpsimd.memset(scales[:].bitcast(I32), 0)
+        wide = sb.tile([P, 4 * S], F32, name="wide", tag="wide", align_bytes=64)
+        lb, e, top = (wide[:, i * S:(i + 1) * S] for i in range(3))
+        nc.vector.memset(scales[:].bitcast(I32), 0)
+        nc.vector.memset(wide[:, 3 * S:], 0.0)
         nc.sync.dma_start(offs_t[:], offs)
+        nc.sync.dma_start(ib_t[:], ib)
+        nc.sync.dma_start(ia_t[:], ia)
+        nc.sync.dma_start(q[:, :32], chg[:, :32])
         nc.sync.dma_start(words[:].bitcast(I32), x_words[0].rearrange("p n t -> p (n t)").bitcast(I32))
+        nc.sync.dma_start(raw["3"][:], w3.rearrange("(p j) c -> p j c", j=PACK))
         for r in range(4):
             nc.scalar.dma_start(scales[r:P:32, :].bitcast(I32), x_scales[0, r:16:4, :].bitcast(I32))
-        for n, w in (("3", w3), ("1", w1), ("2", w2)):
-            nc.sync.dma_start(raw[n][:], w.rearrange("(p j) c -> p j c", j=PACK))
-        nc.sync.dma_start(ia_t[:], ia)
-        nc.sync.dma_start(q[:], chg)
-        nc.sync.dma_start(ib_t[:], ib)
-
-        xs = sb.tile([P, S], U8, name="xs", align_bytes=64)
-        xw = sb.tile([P, S], U32, name="xw", align_bytes=64)
-        nc.vector.tensor_copy(xs[:], scales[:].indirect(offs_t[:]))
-        nc.vector.tensor_copy(xw[:], words[:].indirect(offs_t[:]))
-
-        acc = {}
-        for n in "312":
-            grouped = sb.tile([P, N, PACK], BF16, name="grouped" + n, align_bytes=64)
-            cast = nc.vector.tensor_copy if n == "2" else nc.scalar.copy
-            cast(grouped[:], raw[n][:].rearrange("p j c -> p c j"))
-            codes = sb.tile([P, N], U32, name="codes" + n, align_bytes=64)
-            plane = sb.tile([P, N], U8, name="plane" + n, align_bytes=64)
-            nc.vector.quantize_mx(out=codes[:].bitcast(FP8X4), scales=plane[:], in_=grouped[:].rearrange("p c j -> p (c j)"))
-            acc[n] = ps.tile([P, S], F32, name="acc" + n)
-            nc.tensor.matmul_mx(out=acc[n][:], lhsT=codes[:].bitcast(FP8X4), lhsT_scale=plane[:],
-                                rhs=xw[:].bitcast(FP8X4), rhs_scale=xs[:], start=True, stop=True)
+        nc.sync.dma_start(raw["1"][:], w1.rearrange("(p j) c -> p j c", j=PACK))
+        nc.sync.dma_start(q[:, 32:], chg[:, 32:])
+        nc.sync.dma_start(raw["2"][:], w2.rearrange("(p j) c -> p j c", j=PACK))
 
         halves = [slice(0, HALF), slice(HALF, U)]
         lists = [slice(0, HALF // 16), slice(HALF // 16, U // 16)]
 
-        def pair(window, op, name):
-            first = f32(name + "_b")
-            both = f32(name)
-            for h in range(2):
-                nc.vector.tensor_copy(first[:, halves[h]], window[:].indirect(ib_t[:, lists[h]]))
-            for h in range(2):
-                nc.vector.tensor_tensor(both[:, halves[h]], window[:].indirect(ia_t[:, lists[h]]), first[:, halves[h]], op)
-            return both
+        xw = sb.tile([P, S], U32, name="xw", align_bytes=64)
+        nc.vector.tensor_copy(xw[:], words[:].indirect(offs_t[:]))
+        codes, plane = {}, {}
 
-        y, z, e, ec, sp, top, lb = (f32(n) for n in ("y", "z", "e", "ec", "sp", "top", "lb"))
-        nc.scalar.activation(e[:], acc["3"][:], ACT.Exp)
-        nc.scalar.copy(y[:], acc["1"][:])
-        nc.scalar.copy(z[:], acc["2"][:])
-        nc.vector.tensor_scalar(ec[:], e[:], EXP_CAP, None, ALU.min)
-        dx = pair(y, ALU.subtract, "dx")
-        for h in halves:
-            nc.scalar.activation(sp[:, h], ec[:, h], ACT.Ln, bias=1.0)
-        for h in halves:
-            nc.vector.tensor_tensor(top[:, h], acc["3"][:, h], sp[:, h], ALU.max)
+        def quantise(n, cast):
+            grouped = sb.tile([P, N, PACK], BF16, name="grouped" + n, align_bytes=64)
+            cast(grouped[:], raw[n][:].rearrange("p j c -> p c j"))
+            codes[n] = sb.tile([P, N], U32, name="codes" + n, align_bytes=64)
+            plane[n] = sb.tile([P, N], U8, name="plane" + n, align_bytes=64)
+            nc.vector.quantize_mx(out=codes[n][:].bitcast(FP8X4), scales=plane[n][:], in_=grouped[:].rearrange("p c j -> p (c j)"))
+
+        xs = []
+        for h, n in enumerate("31"):
+            quantise(n, nc.scalar.copy)
+            xs.append(sb.tile([P, HALF], U8, name="xs" + str(h), tag="raw" + n, align_bytes=64))
+            nc.vector.tensor_copy(xs[h][:], scales[:].indirect(offs_t[:, lists[h]]))
+        quantise("2", nc.vector.tensor_copy)
+
+        acc = {}
+        for n, h in (("3", 0), ("1", 0), ("3", 1), ("1", 1), ("2", 0), ("2", 1)):
+            acc[n, h] = ps.tile([P, HALF], F32, name="acc" + n + str(h))
+            nc.tensor.matmul_mx(out=acc[n, h][:], lhsT=codes[n][:].bitcast(FP8X4), lhsT_scale=plane[n][:],
+                                rhs=xw[:, halves[h]].bitcast(FP8X4), rhs_scale=xs[h][:], start=True, stop=True)
+
+        def fetch(window, firsts):
+            for h in range(2):
+                nc.vector.tensor_copy(firsts[h][:], window[:].indirect(ib_t[:, lists[h]]))
+
+        def combine(boths, window, firsts, op):
+            for h in range(2):
+                nc.vector.tensor_tensor(boths[h][:], window[:].indirect(ia_t[:, lists[h]]), firsts[h][:], op)
+
+        def half_tiles(name, tag=None):
+            return [sb.tile([P, HALF], F32, name=name + str(h), tag=(tag or name) + str(h), align_bytes=64) for h in range(2)]
+
+        y = f32("y")
+        for h in range(2):
+            nc.scalar.activation(e[:, halves[h]], acc["3", h][:], ACT.Exp)
+            nc.scalar.copy(y[:, halves[h]], acc["1", h][:])
+        qb = half_tiles("qb")
+        fetch(q, qb)
+        ec = sb.tile([P, S], F32, name="ec", tag="ec", align_bytes=64)
+        nc.vector.tensor_scalar(ec[:], e, EXP_CAP, 1.0, ALU.min, ALU.add)
+        yb = half_tiles("yb")
+        fetch(y, yb)
+        sp = half_tiles("sp")
+        for h in range(2):
+            nc.scalar.activation(sp[h][:], ec[:, halves[h]], ACT.Ln)
+        z = sb.tile([P, S], F32, name="z", tag="ec", align_bytes=64)
+        for h in range(2):
+            nc.scalar.copy(z[:, halves[h]], acc["2", h][:])
+        for h in range(2):
+            nc.vector.tensor_tensor(top[:, halves[h]], acc["3", h][:], sp[h][:], ALU.max)
         for h in halves:
             nc.scalar.activation(lb[:, h], top[:, h], ACT.Ln, bias=0.4)
-        dy = pair(z, ALU.subtract, "dy")
-        s = pair(lb, ALU.add, "s")
-
-        dx2, dy2, rsq, inv, t, v, w, fsq, r, res = (
-            f32(n) for n in ("dx2", "dy2", "rsq", "inv", "t", "v", "w", "fsq", "r", "res"))
-        nc.scalar.activation(dx2[:], dx[:], ACT.Square)
-        nc.scalar.activation(dy2[:], dy[:], ACT.Square)
-        nc.vector.scalar_tensor_tensor(rsq[:], dx2[:], 0.1, dy2[:], ALU.add, ALU.add)
+        dx = half_tiles("dx", "sp")
+        combine(dx, y, yb, ALU.subtract)
+        ra, rb, dx2, ssq, root, t, u, r, res = (f32(n) for n in ("ra", "rb", "dx2", "ssq", "root", "t", "u", "r", "res"))
+        nc.scalar.activation(ra[:], wide[:].indirect(ia_t[:]), ACT.Exp, scale=-0.5)
+        nc.scalar.activation(rb[:], wide[:].indirect(ib_t[:]), ACT.Exp, scale=-0.5)
+        zb = half_tiles("zb", "yb")
+        fetch(z, zb)
+        dy = half_tiles("dy")
+        combine(dy, z, zb, ALU.subtract)
+        for h in range(2):
+            nc.vector.tensor_tensor(dx2[:, halves[h]], dx[h][:], dx[h][:], ALU.mult)
+        dy2 = sb.tile([P, U], F32, name="dy2", tag="wide", align_bytes=64)
+        for h in range(2):
+            nc.scalar.activation(dy2[:, halves[h]], dy[h][:], ACT.Square)
         for h in halves:
-            nc.scalar.activation(inv[:, h], s[:, h], ACT.Exp, scale=-1.0)
+            nc.vector.tensor_tensor(root[:, h], ra[:, h], rb[:, h], ALU.mult)
+        inv = half_tiles("inv")
+        for h in range(2):
+            nc.scalar.activation(inv[h][:], root[:, halves[h]], ACT.Square)
         for h in halves:
-            nc.vector.scalar_tensor_tensor(t[:, h], rsq[:, h], -0.25, inv[:, h], ALU.mult, ALU.mult)
-        for h in halves:
-            nc.vector.tensor_tensor(v[:, h], t[:, h], s[:, h], ALU.add)
-        for h in halves:
-            nc.scalar.activation(w[:, h], v[:, h], ACT.Exp)
-        for h in halves:
-            nc.vector.tensor_tensor(fsq[:, h], w[:, h], rsq[:, h], ALU.add)
-        qq = pair(q, ALU.mult, "qq")
-        for h in halves:
-            nc.scalar.activation(r[:, h], fsq[:, h], ACT.Abs_reciprocal_sqrt)
-            nc.vector.scalar_tensor_tensor(res[:, h], r[:, h], -1.0, qq[:, h], ALU.mult, ALU.mult)
-            nc.sync.dma_start(out[:, h], res[:, h])
+            nc.vector.tensor_tensor(ssq[:, h], dx2[:, h], dy2[:, h], ALU.add)
+        for h in range(2):
+            nc.vector.scalar_tensor_tensor(t[:, halves[h]], ssq[:, halves[h]], 0.1, inv[h][:], ALU.add, ALU.mult)
+        ex = half_tiles("ex")
+        for h in range(2):
+            nc.scalar.activation(ex[h][:], t[:, halves[h]], ACT.Exp, scale=-0.25)
+        p1 = half_tiles("p1", "inv")
+        for h in range(2):
+            nc.vector.scalar_tensor_tensor(p1[h][:], root[:, halves[h]], -1.0, qb[h][:], ALU.mult, ALU.mult)
+        for h in range(2):
+            nc.vector.tensor_tensor(u[:, halves[h]], t[:, halves[h]], ex[h][:], ALU.add)
+        pre = half_tiles("pre", "ex")
+        combine(pre, q, p1, ALU.mult)
+        for h in range(2):
+            nc.scalar.activation(r[:, halves[h]], u[:, halves[h]], ACT.Abs_reciprocal_sqrt)
+            nc.vector.tensor_tensor(res[:, halves[h]], r[:, halves[h]], pre[h][:], ALU.mult)
+            nc.sync.dma_start(out[:, halves[h]], res[:, halves[h]])

@@ -42,44 +42,47 @@ def tile_picked_ygborn_en_p_kernel(tc, x_words, x_scales, w1, w2, w3, chg, offs,
         lb, e, top = (wide[:, i * S:(i + 1) * S] for i in range(3))
         nc.vector.memset(scales[:].bitcast(I32), 0)
         nc.vector.memset(wide[:, 3 * S:], 0.0)
+        def load_weight(n, w):
+            nc.sync.dma_start(raw[n][:], w.rearrange("(p j) c -> p j c", j=PACK))
+
         nc.sync.dma_start(offs_t[:], offs)
+        load_weight("3", w3)
         nc.sync.dma_start(ib_t[:], ib)
-        nc.sync.dma_start(ia_t[:], ia)
-        nc.sync.dma_start(q[:, :32], chg[:, :32])
-        nc.sync.dma_start(words[:].bitcast(I32), x_words[0].rearrange("p n t -> p (n t)").bitcast(I32))
-        nc.sync.dma_start(raw["3"][:], w3.rearrange("(p j) c -> p j c", j=PACK))
         for r in range(4):
-            nc.scalar.dma_start(scales[r:P:32, :].bitcast(I32), x_scales[0, r:16:4, :].bitcast(I32))
-        nc.sync.dma_start(raw["1"][:], w1.rearrange("(p j) c -> p j c", j=PACK))
-        nc.sync.dma_start(q[:, 32:], chg[:, 32:])
-        nc.sync.dma_start(raw["2"][:], w2.rearrange("(p j) c -> p j c", j=PACK))
+            queue = nc.scalar if r < 2 else nc.sync
+            queue.dma_start(scales[r:P:32, :].bitcast(I32), x_scales[0, r:16:4, :].bitcast(I32))
+        nc.sync.dma_start(words[:].bitcast(I32), x_words[0].rearrange("p n t -> p (n t)").bitcast(I32))
+        load_weight("1", w1)
+        load_weight("2", w2)
+        nc.sync.dma_start(q[:], chg)
+        nc.sync.dma_start(ia_t[:], ia)
 
         halves = [slice(0, HALF), slice(HALF, U)]
         lists = [slice(0, HALF // 16), slice(HALF // 16, U // 16)]
-
-        xw = sb.tile([P, S], U32, name="xw", align_bytes=64)
-        nc.vector.tensor_copy(xw[:], words[:].indirect(offs_t[:]))
         codes, plane = {}, {}
 
         def quantise(n, cast):
-            grouped = sb.tile([P, N, PACK], BF16, name="grouped" + n, align_bytes=64)
+            grouped = sb.tile([P, N, PACK], BF16, name="grouped" + n, tag="grouped" + n, align_bytes=64)
             cast(grouped[:], raw[n][:].rearrange("p j c -> p c j"))
             codes[n] = sb.tile([P, N], U32, name="codes" + n, align_bytes=64)
             plane[n] = sb.tile([P, N], U8, name="plane" + n, align_bytes=64)
             nc.vector.quantize_mx(out=codes[n][:].bitcast(FP8X4), scales=plane[n][:], in_=grouped[:].rearrange("p c j -> p (c j)"))
 
-        xs = []
-        for h, n in enumerate("31"):
-            quantise(n, nc.scalar.copy)
-            xs.append(sb.tile([P, HALF], U8, name="xs" + str(h), tag="raw" + n, align_bytes=64))
-            nc.vector.tensor_copy(xs[h][:], scales[:].indirect(offs_t[:, lists[h]]))
-        quantise("2", nc.vector.tensor_copy)
+        xs = sb.tile([P, S], U8, name="xs", align_bytes=64)
+        nc.vector.tensor_copy(xs[:], scales[:].indirect(offs_t[:]))
+        quantise("3", nc.scalar.copy)
+        xw = sb.tile([P, S], U32, name="xw", align_bytes=64)
+        for h in range(2):
+            nc.vector.tensor_copy(xw[:, halves[h]], words[:].indirect(offs_t[:, lists[h]]))
+        quantise("1", nc.scalar.copy)
+        quantise("2", nc.scalar.copy)
 
         acc = {}
-        for n, h in (("3", 0), ("1", 0), ("3", 1), ("1", 1), ("2", 0), ("2", 1)):
-            acc[n, h] = ps.tile([P, HALF], F32, name="acc" + n + str(h))
-            nc.tensor.matmul_mx(out=acc[n, h][:], lhsT=codes[n][:].bitcast(FP8X4), lhsT_scale=plane[n][:],
-                                rhs=xw[:, halves[h]].bitcast(FP8X4), rhs_scale=xs[h][:], start=True, stop=True)
+        for n in "312":
+            for h in range(2):
+                acc[n, h] = ps.tile([P, HALF], F32, name="acc" + n + str(h))
+                nc.tensor.matmul_mx(out=acc[n, h][:], lhsT=codes[n][:].bitcast(FP8X4), lhsT_scale=plane[n][:],
+                                    rhs=xw[:, halves[h]].bitcast(FP8X4), rhs_scale=xs[:, halves[h]], start=True, stop=True)
 
         def fetch(window, firsts):
             for h in range(2):
@@ -95,8 +98,10 @@ def tile_picked_ygborn_en_p_kernel(tc, x_words, x_scales, w1, w2, w3, chg, offs,
         y = f32("y")
         for h in range(2):
             nc.scalar.activation(e[:, halves[h]], acc["3", h][:], ACT.Exp)
+        for h in range(2):
             nc.scalar.copy(y[:, halves[h]], acc["1", h][:])
-        qb = half_tiles("qb")
+        qb_whole = sb.tile([P, U], F32, name="qb", tag="grouped1", align_bytes=64)
+        qb = [qb_whole[:, h] for h in halves]
         fetch(q, qb)
         ec = sb.tile([P, S], F32, name="ec", tag="ec", align_bytes=64)
         nc.vector.tensor_scalar(ec[:], e, EXP_CAP, 1.0, ALU.min, ALU.add)
@@ -112,27 +117,27 @@ def tile_picked_ygborn_en_p_kernel(tc, x_words, x_scales, w1, w2, w3, chg, offs,
             nc.vector.tensor_tensor(top[:, halves[h]], acc["3", h][:], sp[h][:], ALU.max)
         for h in halves:
             nc.scalar.activation(lb[:, h], top[:, h], ACT.Ln, bias=0.4)
-        dx = half_tiles("dx", "sp")
+        dx = [sb.tile([P, HALF], F32, name="dx0", align_bytes=64),
+              sb.tile([P, HALF], F32, name="dx1", tag="sp1", align_bytes=64)]
         combine(dx, y, yb, ALU.subtract)
         ra, rb, dx2, ssq, root, t, u, r, res = (f32(n) for n in ("ra", "rb", "dx2", "ssq", "root", "t", "u", "r", "res"))
         nc.scalar.activation(ra[:], wide[:].indirect(ia_t[:]), ACT.Exp, scale=-0.5)
         nc.scalar.activation(rb[:], wide[:].indirect(ib_t[:]), ACT.Exp, scale=-0.5)
         zb = half_tiles("zb", "yb")
         fetch(z, zb)
-        dy = half_tiles("dy")
+        dy_whole = f32("dy")
+        dy = [dy_whole[:, h] for h in halves]
         combine(dy, z, zb, ALU.subtract)
         for h in range(2):
-            nc.vector.tensor_tensor(dx2[:, halves[h]], dx[h][:], dx[h][:], ALU.mult)
-        dy2 = sb.tile([P, U], F32, name="dy2", tag="wide", align_bytes=64)
-        for h in range(2):
-            nc.scalar.activation(dy2[:, halves[h]], dy[h][:], ACT.Square)
+            nc.gpsimd.tensor_tensor(dx2[:, halves[h]], dx[h][:], dx[h][:], ALU.mult)
+        dy2 = f32("dy2")
+        nc.vector.tensor_tensor(dy2[:], dy_whole[:], dy_whole[:], ALU.mult)
+        nc.vector.tensor_tensor(ssq[:], dx2[:], dy2[:], ALU.add)
         for h in halves:
             nc.vector.tensor_tensor(root[:, h], ra[:, h], rb[:, h], ALU.mult)
         inv = half_tiles("inv")
         for h in range(2):
             nc.scalar.activation(inv[h][:], root[:, halves[h]], ACT.Square)
-        for h in halves:
-            nc.vector.tensor_tensor(ssq[:, h], dx2[:, h], dy2[:, h], ALU.add)
         for h in range(2):
             nc.vector.scalar_tensor_tensor(t[:, halves[h]], ssq[:, halves[h]], 0.1, inv[h][:], ALU.add, ALU.mult)
         ex = half_tiles("ex")

@@ -53,9 +53,9 @@ def tile_picked_ygborn_en_p_kernel(tc, x_words, x_scales, w1, w2, w3, chg, offs,
             queue.dma_start(scales[r:P:32, :].bitcast(I32), x_scales[0, r:16:4, :].bitcast(I32))
         nc.sync.dma_start(words[:].bitcast(I32), x_words[0].rearrange("p n t -> p (n t)").bitcast(I32))
         load_weight("1", w1)
-        load_weight("2", w2)
         nc.sync.dma_start(q[:], chg)
         nc.sync.dma_start(ia_t[:], ia)
+        load_weight("2", w2)
 
         halves = [slice(0, HALF), slice(HALF, U)]
         lists = [slice(0, HALF // 16), slice(HALF // 16, U // 16)]
@@ -75,7 +75,7 @@ def tile_picked_ygborn_en_p_kernel(tc, x_words, x_scales, w1, w2, w3, chg, offs,
         for h in range(2):
             nc.vector.tensor_copy(xw[:, halves[h]], words[:].indirect(offs_t[:, lists[h]]))
         quantise("1", nc.scalar.copy)
-        quantise("2", nc.scalar.copy)
+        quantise("2", nc.vector.tensor_copy)
 
         acc = {}
         for n in "312":
@@ -117,27 +117,27 @@ def tile_picked_ygborn_en_p_kernel(tc, x_words, x_scales, w1, w2, w3, chg, offs,
             nc.vector.tensor_tensor(top[:, halves[h]], acc["3", h][:], sp[h][:], ALU.max)
         for h in halves:
             nc.scalar.activation(lb[:, h], top[:, h], ACT.Ln, bias=0.4)
-        dx = [sb.tile([P, HALF], F32, name="dx0", align_bytes=64),
-              sb.tile([P, HALF], F32, name="dx1", tag="sp1", align_bytes=64)]
+        dx = half_tiles("dx", "sp")
         combine(dx, y, yb, ALU.subtract)
         ra, rb, dx2, ssq, root, t, u, r, res = (f32(n) for n in ("ra", "rb", "dx2", "ssq", "root", "t", "u", "r", "res"))
         nc.scalar.activation(ra[:], wide[:].indirect(ia_t[:]), ACT.Exp, scale=-0.5)
         nc.scalar.activation(rb[:], wide[:].indirect(ib_t[:]), ACT.Exp, scale=-0.5)
         zb = half_tiles("zb", "yb")
         fetch(z, zb)
-        dy_whole = f32("dy")
-        dy = [dy_whole[:, h] for h in halves]
+        dy = half_tiles("dy")
         combine(dy, z, zb, ALU.subtract)
         for h in range(2):
-            nc.gpsimd.tensor_tensor(dx2[:, halves[h]], dx[h][:], dx[h][:], ALU.mult)
+            nc.vector.tensor_tensor(dx2[:, halves[h]], dx[h][:], dx[h][:], ALU.mult)
         dy2 = f32("dy2")
-        nc.vector.tensor_tensor(dy2[:], dy_whole[:], dy_whole[:], ALU.mult)
-        nc.vector.tensor_tensor(ssq[:], dx2[:], dy2[:], ALU.add)
+        for h in range(2):
+            nc.vector.tensor_tensor(dy2[:, halves[h]], dy[h][:], dy[h][:], ALU.mult)
         for h in halves:
             nc.vector.tensor_tensor(root[:, h], ra[:, h], rb[:, h], ALU.mult)
         inv = half_tiles("inv")
         for h in range(2):
             nc.scalar.activation(inv[h][:], root[:, halves[h]], ACT.Square)
+        for h in halves:
+            nc.vector.tensor_tensor(ssq[:, h], dx2[:, h], dy2[:, h], ALU.add)
         for h in range(2):
             nc.vector.scalar_tensor_tensor(t[:, halves[h]], ssq[:, halves[h]], 0.1, inv[h][:], ALU.add, ALU.mult)
         ex = half_tiles("ex")

@@ -53,9 +53,9 @@ def tile_picked_ygborn_en_p_kernel(tc, x_words, x_scales, w1, w2, w3, chg, offs,
             queue.dma_start(scales[r:P:32, :].bitcast(I32), x_scales[0, r:16:4, :].bitcast(I32))
         nc.sync.dma_start(words[:].bitcast(I32), x_words[0].rearrange("p n t -> p (n t)").bitcast(I32))
         load_weight("1", w1)
+        load_weight("2", w2)
         nc.sync.dma_start(q[:], chg)
         nc.sync.dma_start(ia_t[:], ia)
-        load_weight("2", w2)
 
         halves = [slice(0, HALF), slice(HALF, U)]
         lists = [slice(0, HALF // 16), slice(HALF // 16, U // 16)]
@@ -75,7 +75,7 @@ def tile_picked_ygborn_en_p_kernel(tc, x_words, x_scales, w1, w2, w3, chg, offs,
         for h in range(2):
             nc.vector.tensor_copy(xw[:, halves[h]], words[:].indirect(offs_t[:, lists[h]]))
         quantise("1", nc.scalar.copy)
-        quantise("2", nc.vector.tensor_copy)
+        quantise("2", nc.scalar.copy)
 
         acc = {}
         for n in "312":
@@ -112,12 +112,13 @@ def tile_picked_ygborn_en_p_kernel(tc, x_words, x_scales, w1, w2, w3, chg, offs,
             nc.scalar.activation(sp[h][:], ec[:, halves[h]], ACT.Ln)
         z = sb.tile([P, S], F32, name="z", tag="ec", align_bytes=64)
         for h in range(2):
-            nc.scalar.copy(z[:, halves[h]], acc["2", h][:])
-        for h in range(2):
             nc.vector.tensor_tensor(top[:, halves[h]], acc["3", h][:], sp[h][:], ALU.max)
+        for h in range(2):
+            nc.vector.tensor_copy(z[:, halves[h]], acc["2", h][:])
         for h in halves:
             nc.scalar.activation(lb[:, h], top[:, h], ACT.Ln, bias=0.4)
-        dx = half_tiles("dx", "sp")
+        dx = [sb.tile([P, HALF], F32, name="dx0", align_bytes=64),
+              sb.tile([P, HALF], F32, name="dx1", tag="sp1", align_bytes=64)]
         combine(dx, y, yb, ALU.subtract)
         ra, rb, dx2, ssq, root, t, u, r, res = (f32(n) for n in ("ra", "rb", "dx2", "ssq", "root", "t", "u", "r", "res"))
         nc.scalar.activation(ra[:], wide[:].indirect(ia_t[:]), ACT.Exp, scale=-0.5)
@@ -126,11 +127,13 @@ def tile_picked_ygborn_en_p_kernel(tc, x_words, x_scales, w1, w2, w3, chg, offs,
         fetch(z, zb)
         dy = half_tiles("dy")
         combine(dy, z, zb, ALU.subtract)
+        qq0 = sb.tile([P, HALF], F32, name="qq0", tag="yb0", align_bytes=64)
+        nc.vector.tensor_tensor(qq0[:], q[:].indirect(ia_t[:, lists[0]]), qb[0][:], ALU.mult)
         for h in range(2):
             nc.vector.tensor_tensor(dx2[:, halves[h]], dx[h][:], dx[h][:], ALU.mult)
-        dy2 = f32("dy2")
+        dy2 = sb.tile([P, U], F32, name="dy2", tag="wide", align_bytes=64)
         for h in range(2):
-            nc.vector.tensor_tensor(dy2[:, halves[h]], dy[h][:], dy[h][:], ALU.mult)
+            nc.scalar.activation(dy2[:, halves[h]], dy[h][:], ACT.Square)
         for h in halves:
             nc.vector.tensor_tensor(root[:, h], ra[:, h], rb[:, h], ALU.mult)
         inv = half_tiles("inv")
@@ -144,13 +147,16 @@ def tile_picked_ygborn_en_p_kernel(tc, x_words, x_scales, w1, w2, w3, chg, offs,
         for h in range(2):
             nc.scalar.activation(ex[h][:], t[:, halves[h]], ACT.Exp, scale=-0.25)
         p1 = half_tiles("p1", "inv")
-        for h in range(2):
-            nc.vector.scalar_tensor_tensor(p1[h][:], root[:, halves[h]], -1.0, qb[h][:], ALU.mult, ALU.mult)
+        for h, charge in enumerate((qq0, qb[1])):
+            nc.vector.scalar_tensor_tensor(p1[h][:], root[:, halves[h]], -1.0, charge[:], ALU.mult, ALU.mult)
         for h in range(2):
             nc.vector.tensor_tensor(u[:, halves[h]], t[:, halves[h]], ex[h][:], ALU.add)
-        pre = half_tiles("pre", "ex")
-        combine(pre, q, p1, ALU.mult)
-        for h in range(2):
-            nc.scalar.activation(r[:, halves[h]], u[:, halves[h]], ACT.Abs_reciprocal_sqrt)
-            nc.vector.tensor_tensor(res[:, halves[h]], r[:, halves[h]], pre[h][:], ALU.mult)
-            nc.sync.dma_start(out[:, halves[h]], res[:, halves[h]])
+        pre1 = sb.tile([P, HALF], F32, name="pre1", tag="ex1", align_bytes=64)
+        nc.vector.tensor_tensor(pre1[:], q[:].indirect(ia_t[:, lists[1]]), p1[1][:], ALU.mult)
+        quarter = HALF // 2
+        for h, factor in enumerate((p1[0], pre1)):
+            for c in range(0, HALF, quarter):
+                cols = slice(h * HALF + c, h * HALF + c + quarter)
+                nc.scalar.activation(r[:, cols], u[:, cols], ACT.Abs_reciprocal_sqrt)
+                nc.vector.tensor_tensor(res[:, cols], r[:, cols], factor[:, c:c + quarter], ALU.mult)
+                nc.sync.dma_start(out[:, cols], res[:, cols])

from contextlib import ExitStack

import concourse.mybir as mybir

K, T, S, N, U = 512, 1024, 512, 128, 512
FLOPS = 3 * 2 * K * N * S

F32 = mybir.dt.float32
BF16 = mybir.dt.bfloat16
I32 = mybir.dt.int32
U32 = mybir.dt.uint32
U16 = mybir.dt.uint16
U8 = mybir.dt.uint8
FP8X4 = mybir.dt.float8_e4m3fn_x4
ALU = mybir.AluOpType
ACT = mybir.ActivationFunctionType

P = 128
PACK = 4
HALF = U // 2
EXP_CAP = 2.0 ** 60


def tile_picked_ygborn_en_p_kernel(tc, x_words, x_scales, w1, w2, w3, chg, offs, ia, ib, out):
    nc = tc.nc
    with ExitStack() as ctx:
        sb = ctx.enter_context(tc.tile_pool(name="sb", bufs=1))
        ps = ctx.enter_context(tc.psum_pool(name="ps", bufs=1))

        def f32(name, width=U):
            return sb.tile([P, width], F32, name=name, align_bytes=64)

        offs_t = sb.tile([P, S // 16], U16, name="offs_t")
        ia_t = sb.tile([P, U // 16], U16, name="ia_t")
        ib_t = sb.tile([P, U // 16], U16, name="ib_t")
        words = sb.tile([P, T], U32, name="words", align_bytes=64)
        scales = sb.tile([P, T], U8, name="scales", align_bytes=64)
        raw = {n: sb.tile([P, PACK, N], F32, name="raw" + n, tag="raw" + n, align_bytes=64) for n in "312"}
        q = f32("q")

        wide = sb.tile([P, 4 * S], F32, name="wide", tag="wide", align_bytes=64)
        lb, e, top = (wide[:, i * S:(i + 1) * S] for i in range(3))
        nc.vector.memset(scales[:].bitcast(I32), 0)
        nc.vector.memset(wide[:, 3 * S:], 0.0)
        def load_weight(n, w):
            nc.sync.dma_start(raw[n][:], w.rearrange("(p j) c -> p j c", j=PACK))

        nc.sync.dma_start(offs_t[:], offs)
        load_weight("3", w3)
        nc.sync.dma_start(ib_t[:], ib)
        for r in range(4):
            queue = nc.scalar if r < 2 else nc.sync
            queue.dma_start(scales[r:P:32, :].bitcast(I32), x_scales[0, r:16:4, :].bitcast(I32))
        nc.sync.dma_start(words[:].bitcast(I32), x_words[0].rearrange("p n t -> p (n t)").bitcast(I32))
        load_weight("1", w1)
        load_weight("2", w2)
        nc.sync.dma_start(q[:], chg)
        nc.sync.dma_start(ia_t[:], ia)

        halves = [slice(0, HALF), slice(HALF, U)]
        lists = [slice(0, HALF // 16), slice(HALF // 16, U // 16)]
        codes, plane = {}, {}

        def quantise(n, cast):
            grouped = sb.tile([P, N, PACK], BF16, name="grouped" + n, tag="grouped" + n, align_bytes=64)
            cast(grouped[:], raw[n][:].rearrange("p j c -> p c j"))
            codes[n] = sb.tile([P, N], U32, name="codes" + n, align_bytes=64)
            plane[n] = sb.tile([P, N], U8, name="plane" + n, align_bytes=64)
            nc.vector.quantize_mx(out=codes[n][:].bitcast(FP8X4), scales=plane[n][:], in_=grouped[:].rearrange("p c j -> p (c j)"))

        xs = sb.tile([P, S], U8, name="xs", align_bytes=64)
        nc.vector.tensor_copy(xs[:], scales[:].indirect(offs_t[:]))
        quantise("3", nc.scalar.copy)
        xw = sb.tile([P, S], U32, name="xw", align_bytes=64)
        for h in range(2):
            nc.vector.tensor_copy(xw[:, halves[h]], words[:].indirect(offs_t[:, lists[h]]))
        quantise("1", nc.scalar.copy)
        quantise("2", nc.scalar.copy)

        acc = {}
        for n in "312":
            for h in range(2):
                acc[n, h] = ps.tile([P, HALF], F32, name="acc" + n + str(h))
                nc.tensor.matmul_mx(out=acc[n, h][:], lhsT=codes[n][:].bitcast(FP8X4), lhsT_scale=plane[n][:],
                                    rhs=xw[:, halves[h]].bitcast(FP8X4), rhs_scale=xs[:, halves[h]], start=True, stop=True)

        def fetch(window, firsts):
            for h in range(2):
                nc.vector.tensor_copy(firsts[h][:], window[:].indirect(ib_t[:, lists[h]]))

        def combine(boths, window, firsts, op):
            for h in range(2):
                nc.vector.tensor_tensor(boths[h][:], window[:].indirect(ia_t[:, lists[h]]), firsts[h][:], op)

        def half_tiles(name, tag=None):
            return [sb.tile([P, HALF], F32, name=name + str(h), tag=(tag or name) + str(h), align_bytes=64) for h in range(2)]

        y = f32("y")
        for h in range(2):
            nc.scalar.activation(e[:, halves[h]], acc["3", h][:], ACT.Exp)
        for h in range(2):
            nc.scalar.copy(y[:, halves[h]], acc["1", h][:])
        qb_whole = sb.tile([P, U], F32, name="qb", tag="grouped1", align_bytes=64)
        qb = [qb_whole[:, h] for h in halves]
        fetch(q, qb)
        ec = sb.tile([P, S], F32, name="ec", tag="ec", align_bytes=64)
        nc.vector.tensor_scalar(ec[:], e, EXP_CAP, 1.0, ALU.min, ALU.add)
        yb = half_tiles("yb")
        fetch(y, yb)
        sp = half_tiles("sp")
        for h in range(2):
            nc.scalar.activation(sp[h][:], ec[:, halves[h]], ACT.Ln)
        z = sb.tile([P, S], F32, name="z", tag="ec", align_bytes=64)
        for h in range(2):
            nc.vector.tensor_tensor(top[:, halves[h]], acc["3", h][:], sp[h][:], ALU.max)
        for h in range(2):
            nc.vector.tensor_copy(z[:, halves[h]], acc["2", h][:])
        for h in halves:
            nc.scalar.activation(lb[:, h], top[:, h], ACT.Ln, bias=0.4)
        dx = [sb.tile([P, HALF], F32, name="dx0", align_bytes=64),
              sb.tile([P, HALF], F32, name="dx1", tag="sp1", align_bytes=64)]
        combine(dx, y, yb, ALU.subtract)
        ra, rb, dx2, ssq, root, t, u, r, res = (f32(n) for n in ("ra", "rb", "dx2", "ssq", "root", "t", "u", "r", "res"))
        nc.scalar.activation(ra[:], wide[:].indirect(ia_t[:]), ACT.Exp, scale=-0.5)
        nc.scalar.activation(rb[:], wide[:].indirect(ib_t[:]), ACT.Exp, scale=-0.5)
        zb = half_tiles("zb", "yb")
        fetch(z, zb)
        dy = half_tiles("dy")
        combine(dy, z, zb, ALU.subtract)
        qq0 = sb.tile([P, HALF], F32, name="qq0", tag="yb0", align_bytes=64)
        nc.vector.tensor_tensor(qq0[:], q[:].indirect(ia_t[:, lists[0]]), qb[0][:], ALU.mult)
        for h in range(2):
            nc.vector.tensor_tensor(dx2[:, halves[h]], dx[h][:], dx[h][:], ALU.mult)
        dy2 = sb.tile([P, U], F32, name="dy2", tag="wide", align_bytes=64)
        for h in range(2):
            nc.scalar.activation(dy2[:, halves[h]], dy[h][:], ACT.Square)
        for h in halves:
            nc.vector.tensor_tensor(root[:, h], ra[:, h], rb[:, h], ALU.mult)
        inv = half_tiles("inv")
        for h in range(2):
            nc.scalar.activation(inv[h][:], root[:, halves[h]], ACT.Square)
        for h in halves:
            nc.vector.tensor_tensor(ssq[:, h], dx2[:, h], dy2[:, h], ALU.add)
        for h in range(2):
            nc.vector.scalar_tensor_tensor(t[:, halves[h]], ssq[:, halves[h]], 0.1, inv[h][:], ALU.add, ALU.mult)
        ex = half_tiles("ex")
        for h in range(2):
            nc.scalar.activation(ex[h][:], t[:, halves[h]], ACT.Exp, scale=-0.25)
        p1 = half_tiles("p1", "inv")
        for h, charge in enumerate((qq0, qb[1])):
            nc.vector.scalar_tensor_tensor(p1[h][:], root[:, halves[h]], -1.0, charge[:], ALU.mult, ALU.mult)
        for h in range(2):
            nc.vector.tensor_tensor(u[:, halves[h]], t[:, halves[h]], ex[h][:], ALU.add)
        pre1 = sb.tile([P, HALF], F32, name="pre1", tag="ex1", align_bytes=64)
        nc.vector.tensor_tensor(pre1[:], q[:].indirect(ia_t[:, lists[1]]), p1[1][:], ALU.mult)
        quarter = HALF // 2
        for h, factor in enumerate((p1[0], pre1)):
            for c in range(0, HALF, quarter):
                cols = slice(h * HALF + c, h * HALF + c + quarter)
                nc.scalar.activation(r[:, cols], u[:, cols], ACT.Abs_reciprocal_sqrt)
                nc.vector.tensor_tensor(res[:, cols], r[:, cols], factor[:, c:c + quarter], ALU.mult)
                nc.sync.dma_start(out[:, cols], res[:, cols])
